import numpy as np
import ml_dtypes


def mxq(x, axis, fmt="e4m3"):
    dtype, down = {"e4m3": (ml_dtypes.float8_e4m3fn, 7), "e5m2": (ml_dtypes.float8_e5m2, 14)}[fmt]
    v = np.moveaxis(np.asarray(x, np.float32).astype(ml_dtypes.bfloat16).astype(np.float64), axis, -1)
    blocks = v.reshape(v.shape[:-1] + (-1, 32))
    amax = np.abs(blocks).max(-1, keepdims=True)
    byte = np.maximum(np.where(amax > 0, np.frexp(amax)[1] - 1 + 127, 0) - down, 1)
    scale = np.exp2(byte - 127.0)
    codes = (blocks / scale).astype(np.float32).astype(dtype).astype(np.float64)
    return np.moveaxis((codes * scale).reshape(v.shape), -1, axis)


WIDE = False


def mx_kscale(k):
    if not WIDE:
        return np.ones(k)
    levels = np.array([10, -10, 5, -5, 0])
    if k % 512:
        return np.exp2(np.random.permutation(np.resize(levels, k // 32))).repeat(32)
    a = np.empty((k // 512, 16))
    for p in range(k // 512):
        a[p, :8] = np.random.permutation(np.resize(levels, 8))
        for g in range(8):
            far = levels[np.abs(levels - a[p, g]) >= 10]
            a[p, g + 8] = far[np.random.randint(len(far))]
    return np.exp2(a.ravel()).repeat(32)


def f64(x):
    return np.asarray(x).astype(np.float64)


def striped(idx):
    return np.tile(idx.reshape(-1, 16).T, (8, 1)).astype(np.uint16)


def unstriped(offs):
    return offs[:16].T.reshape(-1).astype(np.int64)


def silu(v):
    return v / (1.0 + np.exp(-np.maximum(v, -700.0)))


K, T, E, C, N = 1024, 512, 4, 256, 256


def by_expert(wq, xq):
    return np.concatenate([wq[e].T @ xq[:, e * C:(e + 1) * C] for e in range(E)], axis=1)


def setup_inputs():
    n = np.random.standard_normal
    s = mx_kscale(K)[:, None]
    first = np.random.permutation(np.repeat(np.arange(E), T // E))
    second = (first + 1 + np.random.permutation(np.repeat(np.arange(E - 1), -(-T // (E - 1)))[:T])) % E
    while np.bincount(second, minlength=E).max() != T // E:
        load = np.bincount(second, minlength=E); hi, lo = int(load.argmax()), int(load.argmin())
        t = np.flatnonzero((second == hi) & (first != lo))[0]; second[t] = lo
    slot_token = np.empty(E * C, np.int64); pos = np.empty((2, T), np.int64); fill = np.zeros(E, np.int64)
    place = np.stack([np.random.permutation(C) for _ in range(E)])
    for r, deal in enumerate((first, second)):
        for t in np.random.permutation(T):
            e = deal[t]; j = e * C + place[e, fill[e]]; fill[e] += 1; slot_token[j] = t; pos[r, t] = j
    g = np.random.uniform(0.2, 0.8, T)
    return {
        "xT": (n((K, T)) * s).astype(np.float32),
        "w": (n((E, K, N)) / np.sqrt(K) / s[None]).astype(np.float32),
        "b": (0.3 * n((N, E))).astype(np.float32),
        "gate": np.stack([np.tile(g, (N, 1)), np.tile(1.0 - g, (N, 1))]).astype(np.float32),
        "offs": striped(slot_token),
        "pos1": striped(pos[0]),
        "pos2": striped(pos[1]),
    }


def reference(xT, w, b, gate, offs, pos1, pos2):
    idx = unstriped(offs)
    xq = mxq(f64(xT)[:, idx], 0, "e4m3")
    y = by_expert(mxq(f64(w), 1, "e4m3"), xq)
    y = silu(y + np.repeat(f64(b), C, axis=1))
    return f64(gate[0]) * y[:, unstriped(pos1)] + f64(gate[1]) * y[:, unstriped(pos2)]

@@ -1,0 +1,138 @@
+import concourse.mybir as mybir
+
+K, T, E, C, N = 1024, 512, 4, 256, 256
+FLOPS = 2 * K * N * E * C
+
+F32 = mybir.dt.float32
+BF16 = mybir.dt.bfloat16
+U32 = mybir.dt.uint32
+I32 = mybir.dt.int32
+U16 = mybir.dt.uint16
+U8 = mybir.dt.uint8
+FP8X4 = mybir.dt.float8_e4m3fn_x4
+MULT, ADD = mybir.AluOpType.mult, mybir.AluOpType.add
+SILU = mybir.ActivationFunctionType.Silu
+
+P = 128
+PACK = 4
+K_PASS = P * PACK
+PASSES = K // K_PASS
+BLOCKS = N // P
+SLOTS = E * C
+HALF = T // 2
+WINDOW = 2048
+
+
+def interleave(copy, out, in_):
+    copy(out.rearrange("p (c i) t -> p c t i", i=4), in_.rearrange("p t (c i) -> p c t i", i=4))
+
+
+def tile_routed_moe_kernel(tc, xT, w, b, gate, offs, pos1, pos2, out):
+    nc = tc.nc
+    with (
+        tc.tile_pool(name="lists", bufs=1) as lists,
+        tc.tile_pool(name="keep", bufs=1) as keep,
+        tc.psum_pool(name="psum", bufs=1) as psum,
+    ):
+        offs_sb = lists.tile([P, SLOTS // 16], U16, name="offs_sb")
+        pos_sb = [lists.tile([P, T // 16], U16, name=f"pos_sb{r}") for r in range(2)]
+
+        x_raw = [keep.tile([P, PACK, T], F32, name=f"x_raw{g}") for g in range(PASSES)]
+        w_raw = [keep.tile([P, PASSES, PACK, N], F32, name=f"w_raw{e}") for e in range(E)]
+        bias = keep.tile([P, BLOCKS, E], F32, name="bias")
+        gates = [keep.tile([P, 2, T], F32, name=f"gates{c}") for c in range(BLOCKS)]
+
+        x_scales = keep.tile([P, WINDOW], U8, name="x_scales", align_bytes=64)
+        nc.gpsimd.memset(x_scales[:], 0)
+        x_codes = [keep.tile([P, WINDOW], I32, name=f"x_codes{g}", align_bytes=64) for g in range(PASSES)]
+        for g in range(PASSES):
+            nc.gpsimd.memset(x_codes[g][:, T:], 0)
+        warm = keep.tile([P, 1], F32, name="warm")
+        nc.gpsimd.memset(warm[:], 0.0)
+        warm_out = keep.tile([P, 1], F32, name="warm_out")
+        nc.scalar.activation(warm_out[:], warm[:], SILU)
+
+        x_dram = [xT[g * K_PASS : (g + 1) * K_PASS, :].rearrange("(p j) n -> p j n", j=PACK) for g in range(PASSES)]
+        for h in range(2):
+            nc.sync.dma_start(x_raw[0][:, :, h * HALF : (h + 1) * HALF], x_dram[0][:, :, h * HALF : (h + 1) * HALF])
+        nc.sync.dma_start(offs_sb[:], offs)
+        nc.sync.dma_start(x_raw[1][:], x_dram[1])
+        for e in range(E):
+            for g in range(PASSES):
+                nc.sync.dma_start(w_raw[e][:, g, :, :], w[e, g * K_PASS : (g + 1) * K_PASS, :].rearrange("(p j) n -> p j n", j=PACK))
+            if e == 0:
+                nc.sync.dma_start(bias[:], b.rearrange("(c p) e -> p c e", p=P))
+        nc.sync.dma_start(pos_sb[0][:], pos1)
+        nc.sync.dma_start(pos_sb[1][:], pos2)
+        for c in range(BLOCKS):
+            nc.sync.dma_start(gates[c][:], gate[:, c * P : (c + 1) * P, :].rearrange("r p t -> p r t"))
+
+        slot_codes = [keep.tile([P, SLOTS], U32, name=f"slot_codes{g}", align_bytes=64) for g in range(PASSES)]
+        slot_scales = keep.tile([P, SLOTS], U8, name="slot_scales", align_bytes=64)
+        sc, ve = nc.scalar.copy, nc.vector.tensor_copy
+        for g, copies in enumerate(((ve, ve), (sc, ve))):
+            for h, copy in enumerate(copies):
+                cols = slice(h * HALF, (h + 1) * HALF)
+                x_bf = keep.tile([P, HALF, PACK], BF16, name=f"x_bf{g}{h}", align_bytes=64)
+                interleave(copy, x_bf[:], x_raw[g][:, :, cols])
+                nc.vector.quantize_mx(
+                    out=x_codes[g][:, cols].bitcast(FP8X4),
+                    scales=x_scales[4 * g :, cols],
+                    in_=x_bf[:].rearrange("p n t -> p (n t)"),
+                )
+            nc.vector.tensor_copy(slot_codes[g][:], x_codes[g][:].bitcast(U32).indirect(offs_sb[:]))
+        nc.vector.tensor_copy(slot_scales[:], x_scales[:].indirect(offs_sb[:]))
+
+        y = [keep.tile([P, SLOTS], F32, name=f"y{c}") for c in range(BLOCKS)]
+        w_codes, w_scales = {}, {}
+
+        def quantise_w(blocks):
+            w_bf = keep.tile([P, len(blocks), PASSES, P, PACK], BF16, name=f"w_bf{len(w_codes)}", align_bytes=64)
+            codes = keep.tile([P, len(blocks), PASSES, P], U32, name=f"w_codes{len(w_codes)}", align_bytes=64)
+            scales = keep.tile([P, len(blocks), PASSES, P], U8, name=f"w_scales{len(w_codes)}", align_bytes=64)
+            for i, (e, c, copy) in enumerate(blocks):
+                for g in range(PASSES):
+                    interleave(copy, w_bf[:, i, g, :, :], w_raw[e][:, g, :, c * P : (c + 1) * P])
+                w_codes[e, c] = codes[:, i, :, :]
+                w_scales[e, c] = scales[:, i, :, :]
+            nc.vector.quantize_mx(
+                out=codes[:].rearrange("p b g n -> p (b g n)").bitcast(FP8X4),
+                scales=scales[:].rearrange("p b g n -> p (b g n)"),
+                in_=w_bf[:].rearrange("p b g n t -> p (b g n t)"),
+            )
+
+        def multiply(e, c):
+            slots = slice(e * C, (e + 1) * C)
+            acc = psum.tile([P, C], F32, name=f"acc{e}{c}")
+            for g in range(PASSES):
+                nc.tensor.matmul_mx(
+                    out=acc[:],
+                    lhsT=w_codes[e, c][:, g, :].bitcast(FP8X4),
+                    lhsT_scale=w_scales[e, c][:, g, :],
+                    rhs=slot_codes[g][:, slots].bitcast(FP8X4),
+                    rhs_scale=slot_scales[4 * g :, slots],
+                    start=(g == 0),
+                    stop=(g == PASSES - 1),
+                )
+            nc.scalar.activation(y[c][:, slots], acc[:], SILU, bias=bias[:, c, e : e + 1])
+
+        def combine(c):
+            parts = []
+            for r in range(2):
+                part = keep.tile([P, T], F32, name=f"part{c}{r}")
+                nc.vector.tensor_tensor(part[:], y[c][:].indirect(pos_sb[r][:]), gates[c][:, r, :], MULT)
+                parts.append(part)
+            total = keep.tile([P, T], F32, name=f"total{c}")
+            nc.vector.tensor_tensor(total[:], parts[0][:], parts[1][:], ADD)
+            nc.sync.dma_start(out[c * P : (c + 1) * P, :], total[:])
+
+        quantise_w([(0, 0, sc), (1, 0, sc), (2, 0, sc), (0, 1, sc)])
+        quantise_w([(3, 0, ve)])
+        for e in range(E):
+            multiply(e, 0)
+        quantise_w([(1, 1, sc), (2, 1, sc)])
+        quantise_w([(3, 1, ve)])
+        for e in range(E):
+            multiply(e, 1)
+        combine(0)
+        combine(1)

@@ -1,4 +1,5 @@
 import concourse.mybir as mybir
+from concourse.masks import make_identity
 
 K, T, E, C, N = 1024, 512, 4, 256, 256
 FLOPS = 2 * K * N * E * C
@@ -20,7 +21,7 @@ PASSES = K // K_PASS
 BLOCKS = N // P
 SLOTS = E * C
 HALF = T // 2
-WINDOW = 2048
+WINDOW = 1376
 
 
 def interleave(copy, out, in_):
@@ -46,11 +47,13 @@ def tile_routed_moe_kernel(tc, xT, w, b, gate, offs, pos1, pos2, out):
         nc.gpsimd.memset(x_scales[:], 0)
         x_codes = [keep.tile([P, WINDOW], I32, name=f"x_codes{g}", align_bytes=64) for g in range(PASSES)]
         for g in range(PASSES):
-            nc.gpsimd.memset(x_codes[g][:, T:], 0)
+            nc.vector.memset(x_codes[g][:, T:], 0)
         warm = keep.tile([P, 1], F32, name="warm")
         nc.gpsimd.memset(warm[:], 0.0)
         warm_out = keep.tile([P, 1], F32, name="warm_out")
         nc.scalar.activation(warm_out[:], warm[:], SILU)
+        identity = keep.tile([P, P], F32, name="identity")
+        make_identity(nc, identity[:])
 
         x_dram = [xT[g * K_PASS : (g + 1) * K_PASS, :].rearrange("(p j) n -> p j n", j=PACK) for g in range(PASSES)]
         for h in range(2):
@@ -86,13 +89,18 @@ def tile_routed_moe_kernel(tc, xT, w, b, gate, offs, pos1, pos2, out):
         y = [keep.tile([P, SLOTS], F32, name=f"y{c}") for c in range(BLOCKS)]
         w_codes, w_scales = {}, {}
 
-        def quantise_w(blocks):
-            w_bf = keep.tile([P, len(blocks), PASSES, P, PACK], BF16, name=f"w_bf{len(w_codes)}", align_bytes=64)
-            codes = keep.tile([P, len(blocks), PASSES, P], U32, name=f"w_codes{len(w_codes)}", align_bytes=64)
-            scales = keep.tile([P, len(blocks), PASSES, P], U8, name=f"w_scales{len(w_codes)}", align_bytes=64)
+        def copy_w(blocks):
+            w_bf = keep.tile([P, len(blocks), PASSES, P, PACK], BF16, name=f"w_bf{blocks[0][0]}{blocks[0][1]}", align_bytes=64)
             for i, (e, c, copy) in enumerate(blocks):
                 for g in range(PASSES):
                     interleave(copy, w_bf[:, i, g, :, :], w_raw[e][:, g, :, c * P : (c + 1) * P])
+            return blocks, w_bf
+
+        def quantise_w(copied):
+            blocks, w_bf = copied
+            codes = keep.tile([P, len(blocks), PASSES, P], U32, name=f"w_codes{blocks[0][0]}{blocks[0][1]}", align_bytes=64)
+            scales = keep.tile([P, len(blocks), PASSES, P], U8, name=f"w_scales{blocks[0][0]}{blocks[0][1]}", align_bytes=64)
+            for i, (e, c, copy) in enumerate(blocks):
                 w_codes[e, c] = codes[:, i, :, :]
                 w_scales[e, c] = scales[:, i, :, :]
             nc.vector.quantize_mx(
@@ -116,23 +124,31 @@ def tile_routed_moe_kernel(tc, xT, w, b, gate, offs, pos1, pos2, out):
                 )
             nc.scalar.activation(y[c][:, slots], acc[:], SILU, bias=bias[:, c, e : e + 1])
 
-        def combine(c):
-            parts = []
-            for r in range(2):
-                part = keep.tile([P, T], F32, name=f"part{c}{r}")
-                nc.vector.tensor_tensor(part[:], y[c][:].indirect(pos_sb[r][:]), gates[c][:, r, :], MULT)
-                parts.append(part)
-            total = keep.tile([P, T], F32, name=f"total{c}")
-            nc.vector.tensor_tensor(total[:], parts[0][:], parts[1][:], ADD)
-            nc.sync.dma_start(out[c * P : (c + 1) * P, :], total[:])
+        def gather(c, r):
+            part = keep.tile([P, T], F32, name=f"part{c}{r}")
+            nc.vector.tensor_tensor(part[:], y[c][:].indirect(pos_sb[r][:]), gates[c][:, r, :], MULT)
+            return part
 
-        quantise_w([(0, 0, sc), (1, 0, sc), (2, 0, sc), (0, 1, sc)])
-        quantise_w([(3, 0, ve)])
+        a = copy_w([(0, 0, sc), (1, 0, sc), (2, 0, sc), (0, 1, sc)])
+        quantise_w(a)
+        last0 = copy_w([(3, 0, ve)])
+        last1 = copy_w([(3, 1, ve)])
+        quantise_w(last0)
         for e in range(E):
             multiply(e, 0)
-        quantise_w([(1, 1, sc), (2, 1, sc)])
-        quantise_w([(3, 1, ve)])
+        quantise_w(copy_w([(1, 1, sc), (2, 1, sc)]))
+        quantise_w(last1)
         for e in range(E):
             multiply(e, 1)
-        combine(0)
-        combine(1)
+
+        total0 = psum.tile([P, T], F32, name="acc00")
+        for r in range(2):
+            nc.tensor.matmul(total0[:], identity[:], gather(0, r)[:], start=(r == 0), stop=(r == 1))
+        total0_sb = keep.tile([P, T], F32, name="total0_sb")
+        nc.scalar.copy(total0_sb[:], total0[:])
+        nc.sync.dma_start(out[:P, :], total0_sb[:])
+
+        parts = [gather(1, r) for r in range(2)]
+        total1_sb = keep.tile([P, T], F32, name="total1_sb")
+        nc.vector.tensor_tensor(total1_sb[:], parts[0][:], parts[1][:], ADD)
+        nc.sync.dma_start(out[P:, :], total1_sb[:])

@@ -6,8 +6,8 @@ FLOPS = 2 * K * N * E * C
 
 F32 = mybir.dt.float32
 BF16 = mybir.dt.bfloat16
-U32 = mybir.dt.uint32
 I32 = mybir.dt.int32
+U32 = mybir.dt.uint32
 U16 = mybir.dt.uint16
 U8 = mybir.dt.uint8
 FP8X4 = mybir.dt.float8_e4m3fn_x4
@@ -35,14 +35,13 @@ def tile_routed_moe_kernel(tc, xT, w, b, gate, offs, pos1, pos2, out):
         tc.tile_pool(name="keep", bufs=1) as keep,
         tc.psum_pool(name="psum", bufs=1) as psum,
     ):
+        sc, ve, gp = nc.scalar.copy, nc.vector.tensor_copy, nc.gpsimd.tensor_copy
         offs_sb = lists.tile([P, SLOTS // 16], U16, name="offs_sb")
         pos_sb = [lists.tile([P, T // 16], U16, name=f"pos_sb{r}") for r in range(2)]
-
         x_raw = [keep.tile([P, PACK, T], F32, name=f"x_raw{g}") for g in range(PASSES)]
         w_raw = [keep.tile([P, PASSES, PACK, N], F32, name=f"w_raw{e}") for e in range(E)]
         bias = keep.tile([P, BLOCKS, E], F32, name="bias")
         gates = [keep.tile([P, 2, T], F32, name=f"gates{c}") for c in range(BLOCKS)]
-
         x_scales = keep.tile([P, WINDOW], U8, name="x_scales", align_bytes=64)
         nc.gpsimd.memset(x_scales[:], 0)
         x_codes = [keep.tile([P, WINDOW], I32, name=f"x_codes{g}", align_bytes=64) for g in range(PASSES)]
@@ -56,15 +55,18 @@ def tile_routed_moe_kernel(tc, xT, w, b, gate, offs, pos1, pos2, out):
         make_identity(nc, identity[:])
 
         x_dram = [xT[g * K_PASS : (g + 1) * K_PASS, :].rearrange("(p j) n -> p j n", j=PACK) for g in range(PASSES)]
-        for h in range(2):
-            nc.sync.dma_start(x_raw[0][:, :, h * HALF : (h + 1) * HALF], x_dram[0][:, :, h * HALF : (h + 1) * HALF])
+        nc.sync.dma_start(x_raw[0][:], x_dram[0])
         nc.sync.dma_start(offs_sb[:], offs)
         nc.sync.dma_start(x_raw[1][:], x_dram[1])
-        for e in range(E):
-            for g in range(PASSES):
-                nc.sync.dma_start(w_raw[e][:, g, :, :], w[e, g * K_PASS : (g + 1) * K_PASS, :].rearrange("(p j) n -> p j n", j=PACK))
-            if e == 0:
-                nc.sync.dma_start(bias[:], b.rearrange("(c p) e -> p c e", p=P))
+        nc.sync.dma_start(w_raw[0][:, 0, :, :], w[0, 0:512, :].rearrange("(p j) n -> p j n", j=PACK))
+        nc.sync.dma_start(w_raw[0][:, 1, :, :], w[0, 512:1024, :].rearrange("(p j) n -> p j n", j=PACK))
+        nc.sync.dma_start(bias[:], b.rearrange("(c p) e -> p c e", p=P))
+        nc.sync.dma_start(w_raw[1][:, 0, :, :], w[1, 0:512, :].rearrange("(p j) n -> p j n", j=PACK))
+        nc.sync.dma_start(w_raw[1][:, 1, :, :], w[1, 512:1024, :].rearrange("(p j) n -> p j n", j=PACK))
+        nc.sync.dma_start(w_raw[2][:, 0, :, :], w[2, 0:512, :].rearrange("(p j) n -> p j n", j=PACK))
+        nc.sync.dma_start(w_raw[2][:, 1, :, :], w[2, 512:1024, :].rearrange("(p j) n -> p j n", j=PACK))
+        nc.sync.dma_start(w_raw[3][:, 0, :, :], w[3, 0:512, :].rearrange("(p j) n -> p j n", j=PACK))
+        nc.sync.dma_start(w_raw[3][:, 1, :, :], w[3, 512:1024, :].rearrange("(p j) n -> p j n", j=PACK))
         nc.sync.dma_start(pos_sb[0][:], pos1)
         nc.sync.dma_start(pos_sb[1][:], pos2)
         for c in range(BLOCKS):
@@ -72,8 +74,7 @@ def tile_routed_moe_kernel(tc, xT, w, b, gate, offs, pos1, pos2, out):
 
         slot_codes = [keep.tile([P, SLOTS], U32, name=f"slot_codes{g}", align_bytes=64) for g in range(PASSES)]
         slot_scales = keep.tile([P, SLOTS], U8, name="slot_scales", align_bytes=64)
-        sc, ve = nc.scalar.copy, nc.vector.tensor_copy
-        for g, copies in enumerate(((ve, ve), (sc, ve))):
+        for g, copies in enumerate(((ve, sc), (sc, sc))):
             for h, copy in enumerate(copies):
                 cols = slice(h * HALF, (h + 1) * HALF)
                 x_bf = keep.tile([P, HALF, PACK], BF16, name=f"x_bf{g}{h}", align_bytes=64)
@@ -89,18 +90,25 @@ def tile_routed_moe_kernel(tc, xT, w, b, gate, offs, pos1, pos2, out):
         y = [keep.tile([P, SLOTS], F32, name=f"y{c}") for c in range(BLOCKS)]
         w_codes, w_scales = {}, {}
 
-        def copy_w(blocks):
-            w_bf = keep.tile([P, len(blocks), PASSES, P, PACK], BF16, name=f"w_bf{blocks[0][0]}{blocks[0][1]}", align_bytes=64)
-            for i, (e, c, copy) in enumerate(blocks):
-                for g in range(PASSES):
-                    interleave(copy, w_bf[:, i, g, :, :], w_raw[e][:, g, :, c * P : (c + 1) * P])
-            return blocks, w_bf
+        def copy_w(tag, blocks):
+            w_bf = keep.tile([P, len(blocks), PASSES, P, PACK], BF16, name=f"w_bf{tag}", align_bytes=64)
+            for i, (e, c, copy, whole) in enumerate(blocks):
+                cols = slice(c * P, (c + 1) * P)
+                if whole:
+                    copy(
+                        w_bf[:, i, :, :, :].rearrange("p g (c i) t -> p g c t i", i=4),
+                        w_raw[e][:, :, :, cols].rearrange("p g t (c i) -> p g c t i", i=4),
+                    )
+                else:
+                    for g in range(PASSES):
+                        interleave(copy, w_bf[:, i, g, :, :], w_raw[e][:, g, :, cols])
+            return tag, blocks, w_bf
 
         def quantise_w(copied):
-            blocks, w_bf = copied
-            codes = keep.tile([P, len(blocks), PASSES, P], U32, name=f"w_codes{blocks[0][0]}{blocks[0][1]}", align_bytes=64)
-            scales = keep.tile([P, len(blocks), PASSES, P], U8, name=f"w_scales{blocks[0][0]}{blocks[0][1]}", align_bytes=64)
-            for i, (e, c, copy) in enumerate(blocks):
+            tag, blocks, w_bf = copied
+            codes = keep.tile([P, len(blocks), PASSES, P], U32, name=f"w_codes{tag}", align_bytes=64)
+            scales = keep.tile([P, len(blocks), PASSES, P], U8, name=f"w_scales{tag}", align_bytes=64)
+            for i, (e, c, copy, whole) in enumerate(blocks):
                 w_codes[e, c] = codes[:, i, :, :]
                 w_scales[e, c] = scales[:, i, :, :]
             nc.vector.quantize_mx(
@@ -109,37 +117,39 @@ def tile_routed_moe_kernel(tc, xT, w, b, gate, offs, pos1, pos2, out):
                 in_=w_bf[:].rearrange("p b g n t -> p (b g n t)"),
             )
 
-        def multiply(e, c):
-            slots = slice(e * C, (e + 1) * C)
-            acc = psum.tile([P, C], F32, name=f"acc{e}{c}")
-            for g in range(PASSES):
-                nc.tensor.matmul_mx(
-                    out=acc[:],
-                    lhsT=w_codes[e, c][:, g, :].bitcast(FP8X4),
-                    lhsT_scale=w_scales[e, c][:, g, :],
-                    rhs=slot_codes[g][:, slots].bitcast(FP8X4),
-                    rhs_scale=slot_scales[4 * g :, slots],
-                    start=(g == 0),
-                    stop=(g == PASSES - 1),
-                )
-            nc.scalar.activation(y[c][:, slots], acc[:], SILU, bias=bias[:, c, e : e + 1])
+        def multiply(c):
+            for e in range(E):
+                slots = slice(e * C, (e + 1) * C)
+                acc = psum.tile([P, C], F32, name=f"acc{e}{c}")
+                for g in range(PASSES):
+                    nc.tensor.matmul_mx(
+                        out=acc[:],
+                        lhsT=w_codes[e, c][:, g, :].bitcast(FP8X4),
+                        lhsT_scale=w_scales[e, c][:, g, :],
+                        rhs=slot_codes[g][:, slots].bitcast(FP8X4),
+                        rhs_scale=slot_scales[4 * g :, slots],
+                        start=(g == 0),
+                        stop=(g == PASSES - 1),
+                    )
+                nc.scalar.activation(y[c][:, slots], acc[:], SILU, bias=bias[:, c, e : e + 1])
 
-        def gather(c, r):
-            part = keep.tile([P, T], F32, name=f"part{c}{r}")
-            nc.vector.tensor_tensor(part[:], y[c][:].indirect(pos_sb[r][:]), gates[c][:, r, :], MULT)
+        g4 = copy_w("4", [(0, 1, sc, True), (0, 0, sc, True)])
+        g2 = copy_w("2", [(2, 0, sc, False), (1, 0, sc, True)])
+        quantise_w(g2)
+        quantise_w(g4)
+        g0 = copy_w("0", [(3, 0, ve, False)])
+        quantise_w(g0)
+        g3 = copy_w("3", [(2, 1, ve, False)])
+        g1 = copy_w("1", [(1, 1, sc, True), (3, 1, sc, False)])
+        quantise_w(g1)
+        multiply(0)
+        quantise_w(g3)
+        multiply(1)
+
+        def gather(c, r, lo=0, hi=T):
+            part = keep.tile([P, hi - lo], F32, name=f"part{c}{r}{lo}")
+            nc.vector.tensor_tensor(part[:], y[c][:].indirect(pos_sb[r][:, lo // 16 : hi // 16]), gates[c][:, r, lo:hi], MULT)
             return part
-
-        a = copy_w([(0, 0, sc), (1, 0, sc), (2, 0, sc), (0, 1, sc)])
-        quantise_w(a)
-        last0 = copy_w([(3, 0, ve)])
-        last1 = copy_w([(3, 1, ve)])
-        quantise_w(last0)
-        for e in range(E):
-            multiply(e, 0)
-        quantise_w(copy_w([(1, 1, sc), (2, 1, sc)]))
-        quantise_w(last1)
-        for e in range(E):
-            multiply(e, 1)
 
         total0 = psum.tile([P, T], F32, name="acc00")
         for r in range(2):
@@ -149,6 +159,6 @@ def tile_routed_moe_kernel(tc, xT, w, b, gate, offs, pos1, pos2, out):
         nc.sync.dma_start(out[:P, :], total0_sb[:])
 
         parts = [gather(1, r) for r in range(2)]
-        total1_sb = keep.tile([P, T], F32, name="total1_sb")
-        nc.vector.tensor_tensor(total1_sb[:], parts[0][:], parts[1][:], ADD)
-        nc.sync.dma_start(out[P:, :], total1_sb[:])
+        total1 = keep.tile([P, T], F32, name="total1")
+        nc.vector.tensor_tensor(total1[:], parts[0][:], parts[1][:], ADD)
+        nc.sync.dma_start(out[P:, :], total1[:])

@@ -22,6 +22,7 @@ BLOCKS = N // P
 SLOTS = E * C
 HALF = T // 2
 WINDOW = 1376
+PE_COLS = 384
 
 
 def interleave(copy, out, in_):
@@ -55,18 +56,22 @@ def tile_routed_moe_kernel(tc, xT, w, b, gate, offs, pos1, pos2, out):
         make_identity(nc, identity[:])
 
         x_dram = [xT[g * K_PASS : (g + 1) * K_PASS, :].rearrange("(p j) n -> p j n", j=PACK) for g in range(PASSES)]
-        nc.sync.dma_start(x_raw[0][:], x_dram[0])
+
+        def load_x(g, lo=0, hi=T):
+            nc.sync.dma_start(x_raw[g][:, :, lo:hi], x_dram[g][:, :, lo:hi])
+
+        def load_w(e, lo=0, hi=N):
+            for g in range(PASSES):
+                nc.sync.dma_start(w_raw[e][:, g, :, lo:hi], w[e, g * K_PASS : (g + 1) * K_PASS, lo:hi].rearrange("(p j) n -> p j n", j=PACK))
+
+        load_x(0)
         nc.sync.dma_start(offs_sb[:], offs)
-        nc.sync.dma_start(x_raw[1][:], x_dram[1])
-        nc.sync.dma_start(w_raw[0][:, 0, :, :], w[0, 0:512, :].rearrange("(p j) n -> p j n", j=PACK))
-        nc.sync.dma_start(w_raw[0][:, 1, :, :], w[0, 512:1024, :].rearrange("(p j) n -> p j n", j=PACK))
+        load_x(1)
+        load_w(0)
+        load_w(1)
+        load_w(2)
+        load_w(3)
         nc.sync.dma_start(bias[:], b.rearrange("(c p) e -> p c e", p=P))
-        nc.sync.dma_start(w_raw[1][:, 0, :, :], w[1, 0:512, :].rearrange("(p j) n -> p j n", j=PACK))
-        nc.sync.dma_start(w_raw[1][:, 1, :, :], w[1, 512:1024, :].rearrange("(p j) n -> p j n", j=PACK))
-        nc.sync.dma_start(w_raw[2][:, 0, :, :], w[2, 0:512, :].rearrange("(p j) n -> p j n", j=PACK))
-        nc.sync.dma_start(w_raw[2][:, 1, :, :], w[2, 512:1024, :].rearrange("(p j) n -> p j n", j=PACK))
-        nc.sync.dma_start(w_raw[3][:, 0, :, :], w[3, 0:512, :].rearrange("(p j) n -> p j n", j=PACK))
-        nc.sync.dma_start(w_raw[3][:, 1, :, :], w[3, 512:1024, :].rearrange("(p j) n -> p j n", j=PACK))
         nc.sync.dma_start(pos_sb[0][:], pos1)
         nc.sync.dma_start(pos_sb[1][:], pos2)
         for c in range(BLOCKS):
@@ -74,47 +79,57 @@ def tile_routed_moe_kernel(tc, xT, w, b, gate, offs, pos1, pos2, out):
 
         slot_codes = [keep.tile([P, SLOTS], U32, name=f"slot_codes{g}", align_bytes=64) for g in range(PASSES)]
         slot_scales = keep.tile([P, SLOTS], U8, name="slot_scales", align_bytes=64)
-        for g, copies in enumerate(((ve, sc), (sc, sc))):
-            for h, copy in enumerate(copies):
-                cols = slice(h * HALF, (h + 1) * HALF)
-                x_bf = keep.tile([P, HALF, PACK], BF16, name=f"x_bf{g}{h}", align_bytes=64)
-                interleave(copy, x_bf[:], x_raw[g][:, :, cols])
+
+        def prepare_x(g, lo, n, copy):
+            x_bf = keep.tile([P, n, PACK], BF16, name=f"x_bf{g}{lo}", align_bytes=64)
+            interleave(copy, x_bf[:], x_raw[g][:, :, lo : lo + n])
+            for a in range(0, n, 256):
+                m = min(256, n - a)
                 nc.vector.quantize_mx(
-                    out=x_codes[g][:, cols].bitcast(FP8X4),
-                    scales=x_scales[4 * g :, cols],
-                    in_=x_bf[:].rearrange("p n t -> p (n t)"),
+                    out=x_codes[g][:, lo + a : lo + a + m].bitcast(FP8X4),
+                    scales=x_scales[4 * g :, lo + a : lo + a + m],
+                    in_=x_bf[:, a : a + m, :].rearrange("p n t -> p (n t)"),
                 )
-            nc.vector.tensor_copy(slot_codes[g][:], x_codes[g][:].bitcast(U32).indirect(offs_sb[:]))
+
+        prepare_x(0, 0, 256, ve)
+        prepare_x(0, 256, 256, sc)
+        nc.vector.tensor_copy(slot_codes[0][:], x_codes[0][:].bitcast(U32).indirect(offs_sb[:]))
+        prepare_x(1, 0, 256, sc)
+        prepare_x(1, 256, 256, sc)
+        nc.vector.tensor_copy(slot_codes[1][:], x_codes[1][:].bitcast(U32).indirect(offs_sb[:]))
         nc.vector.tensor_copy(slot_scales[:], x_scales[:].indirect(offs_sb[:]))
 
         y = [keep.tile([P, SLOTS], F32, name=f"y{c}") for c in range(BLOCKS)]
-        w_codes, w_scales = {}, {}
+        groups = {
+            0: [(3, 0)],
+            1: [(1, 1), (3, 1)],
+            2: [(2, 0), (1, 0)],
+            3: [(2, 1)],
+            4: [(0, 1), (0, 0)],
+        }
+        w_bf, w_codes, w_scales, w_to = {}, {}, {}, {}
+        for i, blocks in groups.items():
+            bf = keep.tile([P, len(blocks), PASSES, P, PACK], BF16, name=f"w_bf{i}", align_bytes=64)
+            codes = keep.tile([P, len(blocks), PASSES, P], U32, name=f"w_codes{i}", align_bytes=64)
+            scales = keep.tile([P, len(blocks), PASSES, P], U8, name=f"w_scales{i}", align_bytes=64)
+            w_bf[i] = (bf, codes, scales)
+            for j, ec in enumerate(blocks):
+                w_to[ec], w_codes[ec], w_scales[ec] = bf[:, j, :, :, :], codes[:, j, :, :], scales[:, j, :, :]
 
-        def copy_w(tag, blocks):
-            w_bf = keep.tile([P, len(blocks), PASSES, P, PACK], BF16, name=f"w_bf{tag}", align_bytes=64)
-            for i, (e, c, copy, whole) in enumerate(blocks):
-                cols = slice(c * P, (c + 1) * P)
-                if whole:
-                    copy(
-                        w_bf[:, i, :, :, :].rearrange("p g (c i) t -> p g c t i", i=4),
-                        w_raw[e][:, :, :, cols].rearrange("p g t (c i) -> p g c t i", i=4),
-                    )
-                else:
-                    for g in range(PASSES):
-                        interleave(copy, w_bf[:, i, g, :, :], w_raw[e][:, g, :, cols])
-            return tag, blocks, w_bf
+        def copy_w(e, c, copy, whole):
+            to, cols = w_to[e, c], slice(c * P, (c + 1) * P)
+            if whole:
+                copy(to.rearrange("p g (c i) t -> p g c t i", i=4), w_raw[e][:, :, :, cols].rearrange("p g t (c i) -> p g c t i", i=4))
+            else:
+                for g in range(PASSES):
+                    interleave(copy, to[:, g, :, :], w_raw[e][:, g, :, cols])
 
-        def quantise_w(copied):
-            tag, blocks, w_bf = copied
-            codes = keep.tile([P, len(blocks), PASSES, P], U32, name=f"w_codes{tag}", align_bytes=64)
-            scales = keep.tile([P, len(blocks), PASSES, P], U8, name=f"w_scales{tag}", align_bytes=64)
-            for i, (e, c, copy, whole) in enumerate(blocks):
-                w_codes[e, c] = codes[:, i, :, :]
-                w_scales[e, c] = scales[:, i, :, :]
+        def quantise_w(i):
+            bf, codes, scales = w_bf[i]
             nc.vector.quantize_mx(
                 out=codes[:].rearrange("p b g n -> p (b g n)").bitcast(FP8X4),
                 scales=scales[:].rearrange("p b g n -> p (b g n)"),
-                in_=w_bf[:].rearrange("p b g n t -> p (b g n t)"),
+                in_=bf[:].rearrange("p b g n t -> p (b g n t)"),
             )
 
         def multiply(c):
@@ -133,17 +148,20 @@ def tile_routed_moe_kernel(tc, xT, w, b, gate, offs, pos1, pos2, out):
                     )
                 nc.scalar.activation(y[c][:, slots], acc[:], SILU, bias=bias[:, c, e : e + 1])
 
-        g4 = copy_w("4", [(0, 1, sc, True), (0, 0, sc, True)])
-        g2 = copy_w("2", [(2, 0, sc, False), (1, 0, sc, True)])
-        quantise_w(g2)
-        quantise_w(g4)
-        g0 = copy_w("0", [(3, 0, ve, False)])
-        quantise_w(g0)
-        g3 = copy_w("3", [(2, 1, ve, False)])
-        g1 = copy_w("1", [(1, 1, sc, True), (3, 1, sc, False)])
-        quantise_w(g1)
+        copy_w(0, 1, sc, True)
+        copy_w(0, 0, sc, True)
+        copy_w(2, 0, sc, False)
+        copy_w(1, 0, sc, True)
+        quantise_w(2)
+        quantise_w(4)
+        copy_w(3, 0, ve, False)
+        quantise_w(0)
+        copy_w(2, 1, ve, False)
+        copy_w(1, 1, sc, True)
+        copy_w(3, 1, sc, False)
+        quantise_w(1)
         multiply(0)
-        quantise_w(g3)
+        quantise_w(3)
         multiply(1)
 
         def gather(c, r, lo=0, hi=T):
@@ -151,14 +169,19 @@ def tile_routed_moe_kernel(tc, xT, w, b, gate, offs, pos1, pos2, out):
             nc.vector.tensor_tensor(part[:], y[c][:].indirect(pos_sb[r][:, lo // 16 : hi // 16]), gates[c][:, r, lo:hi], MULT)
             return part
 
-        total0 = psum.tile([P, T], F32, name="acc00")
+        total0_psum = psum.tile([P, PE_COLS], F32, name="acc00")
+        parts0 = []
         for r in range(2):
-            nc.tensor.matmul(total0[:], identity[:], gather(0, r)[:], start=(r == 0), stop=(r == 1))
-        total0_sb = keep.tile([P, T], F32, name="total0_sb")
-        nc.scalar.copy(total0_sb[:], total0[:])
-        nc.sync.dma_start(out[:P, :], total0_sb[:])
+            parts0.append(gather(0, r))
+            nc.tensor.matmul(total0_psum[:], identity[:], parts0[r][:, :PE_COLS], start=(r == 0), stop=(r == 1))
+        total0 = keep.tile([P, T], F32, name="total0")
+        nc.scalar.copy(total0[:, :PE_COLS], total0_psum[:])
 
-        parts = [gather(1, r) for r in range(2)]
-        total1 = keep.tile([P, T], F32, name="total1")
-        nc.vector.tensor_tensor(total1[:], parts[0][:], parts[1][:], ADD)
-        nc.sync.dma_start(out[P:, :], total1[:])
+        first = gather(1, 0)
+        nc.vector.tensor_tensor(total0[:, PE_COLS:], parts0[0][:, PE_COLS:], parts0[1][:, PE_COLS:], ADD)
+        nc.sync.dma_start(out[:P, :], total0[:])
+        seconds = [gather(1, 1, lo, lo + HALF) for lo in (0, HALF)]
+        for i, lo in enumerate((0, HALF)):
+            total1 = keep.tile([P, HALF], F32, name=f"total1{i}")
+            nc.vector.tensor_tensor(total1[:], first[:, lo : lo + HALF], seconds[i][:], ADD)
+            nc.sync.dma_start(out[P:, lo : lo + HALF], total1[:])

import concourse.mybir as mybir
from concourse.masks import make_identity

K, T, E, C, N = 1024, 512, 4, 256, 256
FLOPS = 2 * K * N * E * C

F32 = mybir.dt.float32
BF16 = mybir.dt.bfloat16
I32 = mybir.dt.int32
U32 = mybir.dt.uint32
U16 = mybir.dt.uint16
U8 = mybir.dt.uint8
FP8X4 = mybir.dt.float8_e4m3fn_x4
MULT, ADD = mybir.AluOpType.mult, mybir.AluOpType.add
SILU = mybir.ActivationFunctionType.Silu

P = 128
PACK = 4
K_PASS = P * PACK
PASSES = K // K_PASS
BLOCKS = N // P
SLOTS = E * C
HALF = T // 2
WINDOW = 1376
PE_COLS = 384


def interleave(copy, out, in_):
    copy(out.rearrange("p (c i) t -> p c t i", i=4), in_.rearrange("p t (c i) -> p c t i", i=4))


def tile_routed_moe_kernel(tc, xT, w, b, gate, offs, pos1, pos2, out):
    nc = tc.nc
    with (
        tc.tile_pool(name="lists", bufs=1) as lists,
        tc.tile_pool(name="keep", bufs=1) as keep,
        tc.psum_pool(name="psum", bufs=1) as psum,
    ):
        sc, ve, gp = nc.scalar.copy, nc.vector.tensor_copy, nc.gpsimd.tensor_copy
        offs_sb = lists.tile([P, SLOTS // 16], U16, name="offs_sb")
        pos_sb = [lists.tile([P, T // 16], U16, name=f"pos_sb{r}") for r in range(2)]
        x_raw = [keep.tile([P, PACK, T], F32, name=f"x_raw{g}") for g in range(PASSES)]
        w_raw = [keep.tile([P, PASSES, PACK, N], F32, name=f"w_raw{e}") for e in range(E)]
        bias = keep.tile([P, BLOCKS, E], F32, name="bias")
        gates = [keep.tile([P, 2, T], F32, name=f"gates{c}") for c in range(BLOCKS)]
        x_scales = keep.tile([P, WINDOW], U8, name="x_scales", align_bytes=64)
        nc.gpsimd.memset(x_scales[:], 0)
        x_codes = [keep.tile([P, WINDOW], I32, name=f"x_codes{g}", align_bytes=64) for g in range(PASSES)]
        for g in range(PASSES):
            nc.vector.memset(x_codes[g][:, T:], 0)
        warm = keep.tile([P, 1], F32, name="warm")
        nc.gpsimd.memset(warm[:], 0.0)
        warm_out = keep.tile([P, 1], F32, name="warm_out")
        nc.scalar.activation(warm_out[:], warm[:], SILU)
        identity = keep.tile([P, P], F32, name="identity")
        make_identity(nc, identity[:])

        x_dram = [xT[g * K_PASS : (g + 1) * K_PASS, :].rearrange("(p j) n -> p j n", j=PACK) for g in range(PASSES)]

        def load_x(g, lo=0, hi=T):
            nc.sync.dma_start(x_raw[g][:, :, lo:hi], x_dram[g][:, :, lo:hi])

        def load_w(e, lo=0, hi=N):
            for g in range(PASSES):
                nc.sync.dma_start(w_raw[e][:, g, :, lo:hi], w[e, g * K_PASS : (g + 1) * K_PASS, lo:hi].rearrange("(p j) n -> p j n", j=PACK))

        load_x(0)
        nc.sync.dma_start(offs_sb[:], offs)
        load_x(1)
        load_w(0)
        load_w(1)
        load_w(2)
        load_w(3)
        nc.sync.dma_start(bias[:], b.rearrange("(c p) e -> p c e", p=P))
        nc.sync.dma_start(pos_sb[0][:], pos1)
        nc.sync.dma_start(pos_sb[1][:], pos2)
        for c in range(BLOCKS):
            nc.sync.dma_start(gates[c][:], gate[:, c * P : (c + 1) * P, :].rearrange("r p t -> p r t"))

        slot_codes = [keep.tile([P, SLOTS], U32, name=f"slot_codes{g}", align_bytes=64) for g in range(PASSES)]
        slot_scales = keep.tile([P, SLOTS], U8, name="slot_scales", align_bytes=64)

        def prepare_x(g, lo, n, copy):
            x_bf = keep.tile([P, n, PACK], BF16, name=f"x_bf{g}{lo}", align_bytes=64)
            interleave(copy, x_bf[:], x_raw[g][:, :, lo : lo + n])
            for a in range(0, n, 256):
                m = min(256, n - a)
                nc.vector.quantize_mx(
                    out=x_codes[g][:, lo + a : lo + a + m].bitcast(FP8X4),
                    scales=x_scales[4 * g :, lo + a : lo + a + m],
                    in_=x_bf[:, a : a + m, :].rearrange("p n t -> p (n t)"),
                )

        prepare_x(0, 0, 256, ve)
        prepare_x(0, 256, 256, sc)
        nc.vector.tensor_copy(slot_codes[0][:], x_codes[0][:].bitcast(U32).indirect(offs_sb[:]))
        prepare_x(1, 0, 256, sc)
        prepare_x(1, 256, 256, sc)
        nc.vector.tensor_copy(slot_codes[1][:], x_codes[1][:].bitcast(U32).indirect(offs_sb[:]))
        nc.vector.tensor_copy(slot_scales[:], x_scales[:].indirect(offs_sb[:]))

        y = [keep.tile([P, SLOTS], F32, name=f"y{c}") for c in range(BLOCKS)]
        groups = {
            0: [(3, 0)],
            1: [(1, 1), (3, 1)],
            2: [(2, 0), (1, 0)],
            3: [(2, 1)],
            4: [(0, 1), (0, 0)],
        }
        w_bf, w_codes, w_scales, w_to = {}, {}, {}, {}
        for i, blocks in groups.items():
            bf = keep.tile([P, len(blocks), PASSES, P, PACK], BF16, name=f"w_bf{i}", align_bytes=64)
            codes = keep.tile([P, len(blocks), PASSES, P], U32, name=f"w_codes{i}", align_bytes=64)
            scales = keep.tile([P, len(blocks), PASSES, P], U8, name=f"w_scales{i}", align_bytes=64)
            w_bf[i] = (bf, codes, scales)
            for j, ec in enumerate(blocks):
                w_to[ec], w_codes[ec], w_scales[ec] = bf[:, j, :, :, :], codes[:, j, :, :], scales[:, j, :, :]

        def copy_w(e, c, copy, whole):
            to, cols = w_to[e, c], slice(c * P, (c + 1) * P)
            if whole:
                copy(to.rearrange("p g (c i) t -> p g c t i", i=4), w_raw[e][:, :, :, cols].rearrange("p g t (c i) -> p g c t i", i=4))
            else:
                for g in range(PASSES):
                    interleave(copy, to[:, g, :, :], w_raw[e][:, g, :, cols])

        def quantise_w(i):
            bf, codes, scales = w_bf[i]
            nc.vector.quantize_mx(
                out=codes[:].rearrange("p b g n -> p (b g n)").bitcast(FP8X4),
                scales=scales[:].rearrange("p b g n -> p (b g n)"),
                in_=bf[:].rearrange("p b g n t -> p (b g n t)"),
            )

        def multiply(c):
            for e in range(E):
                slots = slice(e * C, (e + 1) * C)
                acc = psum.tile([P, C], F32, name=f"acc{e}{c}")
                for g in range(PASSES):
                    nc.tensor.matmul_mx(
                        out=acc[:],
                        lhsT=w_codes[e, c][:, g, :].bitcast(FP8X4),
                        lhsT_scale=w_scales[e, c][:, g, :],
                        rhs=slot_codes[g][:, slots].bitcast(FP8X4),
                        rhs_scale=slot_scales[4 * g :, slots],
                        start=(g == 0),
                        stop=(g == PASSES - 1),
                    )
                nc.scalar.activation(y[c][:, slots], acc[:], SILU, bias=bias[:, c, e : e + 1])

        copy_w(0, 1, sc, True)
        copy_w(0, 0, sc, True)
        copy_w(2, 0, sc, False)
        copy_w(1, 0, sc, True)
        quantise_w(2)
        quantise_w(4)
        copy_w(3, 0, ve, False)
        quantise_w(0)
        copy_w(2, 1, ve, False)
        copy_w(1, 1, sc, True)
        copy_w(3, 1, sc, False)
        quantise_w(1)
        multiply(0)
        quantise_w(3)
        multiply(1)

        def gather(c, r, lo=0, hi=T):
            part = keep.tile([P, hi - lo], F32, name=f"part{c}{r}{lo}")
            nc.vector.tensor_tensor(part[:], y[c][:].indirect(pos_sb[r][:, lo // 16 : hi // 16]), gates[c][:, r, lo:hi], MULT)
            return part

        total0_psum = psum.tile([P, PE_COLS], F32, name="acc00")
        parts0 = []
        for r in range(2):
            parts0.append(gather(0, r))
            nc.tensor.matmul(total0_psum[:], identity[:], parts0[r][:, :PE_COLS], start=(r == 0), stop=(r == 1))
        total0 = keep.tile([P, T], F32, name="total0")
        nc.scalar.copy(total0[:, :PE_COLS], total0_psum[:])

        first = gather(1, 0)
        nc.vector.tensor_tensor(total0[:, PE_COLS:], parts0[0][:, PE_COLS:], parts0[1][:, PE_COLS:], ADD)
        nc.sync.dma_start(out[:P, :], total0[:])
        seconds = [gather(1, 1, lo, lo + HALF) for lo in (0, HALF)]
        for i, lo in enumerate((0, HALF)):
            total1 = keep.tile([P, HALF], F32, name=f"total1{i}")
            nc.vector.tensor_tensor(total1[:], first[:, lo : lo + HALF], seconds[i][:], ADD)
            nc.sync.dma_start(out[P:, lo : lo + HALF], total1[:])
